import numpy as np
import ml_dtypes


def mxq(x, axis, fmt="e4m3"):
    dtype, down = {"e4m3": (ml_dtypes.float8_e4m3fn, 7), "e5m2": (ml_dtypes.float8_e5m2, 14)}[fmt]
    v = np.moveaxis(np.asarray(x, np.float32).astype(ml_dtypes.bfloat16).astype(np.float64), axis, -1)
    blocks = v.reshape(v.shape[:-1] + (-1, 32))
    amax = np.abs(blocks).max(-1, keepdims=True)
    byte = np.maximum(np.where(amax > 0, np.frexp(amax)[1] - 1 + 127, 0) - down, 1)
    scale = np.exp2(byte - 127.0)
    codes = (blocks / scale).astype(np.float32).astype(dtype).astype(np.float64)
    return np.moveaxis((codes * scale).reshape(v.shape), -1, axis)


WIDE = False


def mx_kscale(k):
    if not WIDE:
        return np.ones(k)
    levels = np.array([10, -10, 5, -5, 0])
    if k % 512:
        return np.exp2(np.random.permutation(np.resize(levels, k // 32))).repeat(32)
    a = np.empty((k // 512, 16))
    for p in range(k // 512):
        a[p, :8] = np.random.permutation(np.resize(levels, 8))
        for g in range(8):
            far = levels[np.abs(levels - a[p, g]) >= 10]
            a[p, g + 8] = far[np.random.randint(len(far))]
    return np.exp2(a.ravel()).repeat(32)


def f64(x):
    return np.asarray(x).astype(np.float64)


def striped(idx):
    return np.tile(np.asarray(idx).reshape(-1, 16).T, (8, 1)).astype(np.uint16)


def unstriped(offs):
    return offs[:16].T.reshape(-1).astype(np.int64)


E2M1 = np.array([0.0, 0.5, 1.0, 1.5, 2.0, 3.0, 4.0, 6.0, -0.0, -0.5, -1.0, -1.5, -2.0, -3.0, -4.0, -6.0])


def pack_weight(w, fmt):
    k, n = w.shape
    w = f64(np.asarray(w, np.float32).astype(ml_dtypes.bfloat16)).reshape(k // 32, 32, n)
    amax = np.abs(w).max(1)
    if fmt == "e4m3":
        byte = np.frexp(amax)[1] - 1 + 127 - 7
    else:
        mant, ex = np.frexp(amax / 6.0)
        byte = np.where(mant > 0.5, ex, ex - 1) + 127
    byte = np.clip(np.where(amax > 0, byte, 1), 1, 254)
    scaled = (w * np.exp2(127.0 - byte)[:, None, :]).reshape(k, n).astype(np.float32)
    by_word = np.ascontiguousarray(scaled.reshape(k // 512, 128, 4, n).transpose(0, 1, 3, 2))
    if fmt == "e4m3":
        words = by_word.astype(ml_dtypes.float8_e4m3fn).view(np.uint8)
    else:
        c = by_word.astype(ml_dtypes.float4_e2m1fn).view(np.uint8) & 0xF
        words = (c[..., 0::2] | (c[..., 1::2] << 4)).reshape(k // 512, 128, 2 * n)
    return np.ascontiguousarray(words), np.ascontiguousarray(byte.astype(np.uint8).reshape(k // 512, 16, n))


def unpack_weight(words, scales, fmt):
    g, _, n = scales.shape
    words = np.ascontiguousarray(words).reshape(g, 128, n, -1)
    if fmt == "e4m3":
        vals = words.view(ml_dtypes.float8_e4m3fn).astype(np.float64)
    else:
        nib = np.empty((g, 128, n, 4), np.uint8)
        nib[..., 0::2] = words & 0xF
        nib[..., 1::2] = words >> 4
        vals = E2M1[nib]
    vals = vals * np.repeat(np.exp2(scales.astype(np.float64) - 127.0), 8, axis=1)[..., None]
    return vals.transpose(0, 1, 3, 2).reshape(g * 512, n)


def sigmoid(v):
    return 1.0 / (1.0 + np.exp(-v))


D, T, I, Q, E, M = 512, 2048, 512, 128, 512, 512


def setup_inputs():
    n = np.random.standard_normal
    idx = np.random.permutation(T)[:I]
    fd = mx_kscale(D)
    fm = mx_kscale(M)
    fi = mx_kscale(I)
    ti = np.ones(T)
    ti[idx] = fi
    keysp = pack_weight(n((D, T)) / fd[:, None], "e4m3")
    return {
        "query": (n((D, Q)) * 0.4 / np.sqrt(D) * fd[:, None]).astype(np.float32),
        "pkey": (n((D, M)) / fd[:, None]).astype(np.float32),
        "pval": (n((M, E)) / fm[:, None]).astype(np.float32),
        "keys_words": keysp[0],
        "keys_scales": keysp[1],
        "vals": (n((E, T)) / ti).astype(np.float32),
        "l1": (np.random.uniform(7.0, 7.6, (Q, 1))).astype(np.float32),
        "l2": (np.random.uniform(7.0, 7.6, (Q, 1))).astype(np.float32),
        "psz": (np.random.uniform(0.5, 2.0, (1, M)) * fm).astype(np.float32),
        "size": (np.random.uniform(0.5, 2.0, (1, I)) * fi).astype(np.float32),
        "offs": striped(idx),
    }


def reference(query, pkey, pval, keys_words, keys_scales, vals, l1, l2, psz, size, offs):
    idx = unstriped(offs)
    keysu = unpack_weight(keys_words, keys_scales, "e4m3")
    queryq = mxq(f64(query), 0, "e4m3")
    pkeyq = mxq(f64(pkey), 0, "e4m3")
    a = queryq.T @ pkeyq
    keysidxg = keysu[:, idx]
    b = queryq.T @ keysidxg
    g = sigmoid(f64(l1) - f64(l2))
    w = np.exp(a - f64(l1)) * g * f64(psz)
    x = np.exp(b - f64(l2)) * (1.0 - g) * f64(size)
    wt = w.T
    xt = x.T
    vt = f64(vals)[:, idx].T
    wtq = mxq(wt, 0, "e4m3")
    pvalq = mxq(f64(pval), 0, "e4m3")
    xtq = mxq(xt, 0, "e4m3")
    vtq = mxq(vt, 0, "e4m3")
    o = wtq.T @ pvalq + xtq.T @ vtq
    return o

@@ -1,0 +1,166 @@
+from contextlib import ExitStack
+
+import concourse.mybir as mybir
+from concourse.masks import make_identity
+
+D, T, I, Q, E, M = 512, 2048, 512, 128, 512, 512
+FLOPS = 2 * Q * (D * M + D * I + M * E + I * E)
+
+F32 = mybir.dt.float32
+BF16 = mybir.dt.bfloat16
+I32 = mybir.dt.int32
+U32 = mybir.dt.uint32
+U16 = mybir.dt.uint16
+U8 = mybir.dt.uint8
+FP8X4 = mybir.dt.float8_e4m3fn_x4
+ALU = mybir.AluOpType
+ACT = mybir.ActivationFunctionType
+
+P = 128
+PACK = 4
+BLOCKS = E // P
+HALF = E // 2
+
+
+def tile_attend_cascade_kernel(tc, query, pkey, pval, keys_words, keys_scales, vals, l1, l2, psz, size, offs, out):
+    nc = tc.nc
+    with ExitStack() as ctx:
+        sb = ctx.enter_context(tc.tile_pool(name="sb", bufs=1))
+        ps = ctx.enter_context(tc.psum_pool(name="ps", bufs=1))
+
+        def weave(copy, raw, name):
+            width = raw.shape[2]
+            woven = sb.tile([P, width * PACK], BF16, name=name + "_woven", align_bytes=64)
+            copy(
+                woven[:].rearrange("p (c i t) -> p c t i", i=4, t=PACK),
+                raw.rearrange("p t (c i) -> p c t i", i=4),
+            )
+            return woven
+
+        def quantize(woven, name):
+            width = woven.shape[1] // PACK
+            codes = sb.tile([P, width], U32, name=name + "_codes", align_bytes=64)
+            scales = sb.tile([P, width], U8, name=name + "_scales", align_bytes=64)
+            nc.vector.quantize_mx(out=codes[:].bitcast(FP8X4), scales=scales[:], in_=woven[:])
+            return codes, scales
+
+        def multiply(acc, lhs, rhs, start, stop):
+            nc.tensor.matmul_mx(
+                out=acc,
+                lhsT=lhs[0][:].bitcast(FP8X4),
+                lhsT_scale=lhs[1][:],
+                rhs=rhs[0][:].bitcast(FP8X4),
+                rhs_scale=rhs[1][:],
+                start=start,
+                stop=stop,
+            )
+
+        offsets = sb.tile([P, I // 16], U16, name="offsets")
+        nc.sync.dma_start(offsets[:], offs)
+        q_raw = sb.tile([P, PACK, Q], F32, name="q_raw")
+        nc.sync.dma_start(q_raw[:], query.rearrange("(p t) q -> p t q", t=PACK))
+        key_pool = sb.tile([P, T], I32, name="key_pool")
+        nc.sync.dma_start(key_pool[:], keys_words[0].rearrange("p n t -> p (n t)").bitcast(I32))
+        pkey_raw = sb.tile([P, PACK, M], F32, name="pkey_raw")
+        nc.sync.dma_start(pkey_raw[:], pkey.rearrange("(p t) m -> p t m", t=PACK))
+
+        scale_pool = sb.tile([P, T], U8, name="scale_pool")
+        nc.vector.memset(scale_pool[:].bitcast(I32), 0)
+        for r in range(4):
+            nc.gpsimd.dma_start(scale_pool[r:P:32, :].bitcast(I32), keys_scales[0, r:16:4, :].bitcast(I32))
+
+        l1_col = sb.tile([P, 1], F32, name="l1_col")
+        nc.scalar.dma_start(l1_col[:], l1)
+        l2_col = sb.tile([P, 1], F32, name="l2_col")
+        nc.scalar.dma_start(l2_col[:], l2)
+        size_col = sb.tile([P, PACK], F32, name="size_col")
+        nc.scalar.dma_start(size_col[:], size.rearrange("o (p t) -> p (o t)", t=PACK))
+        psz_col = sb.tile([P, PACK], F32, name="psz_col")
+        nc.scalar.dma_start(psz_col[:], psz.rearrange("o (p t) -> p (o t)", t=PACK))
+
+        val_pool = []
+        for b in range(BLOCKS):
+            pool_b = sb.tile([P, T], F32, name="val_pool%d" % b)
+            nc.sync.dma_start(pool_b[:], vals[b * P : (b + 1) * P, :])
+            val_pool.append(pool_b)
+        pval_rows = pval.rearrange("(p t) e -> p t e", t=PACK)
+        pval_raw = []
+        for h in range(2):
+            raw_h = sb.tile([P, PACK, HALF], F32, name="pval_raw%d" % h)
+            nc.sync.dma_start(raw_h[:], pval_rows[:, :, h * HALF : (h + 1) * HALF])
+            pval_raw.append(raw_h)
+
+        ident = sb.tile([P, P], F32, name="ident")
+        make_identity(nc, ident[:])
+
+        q_mx = quantize(weave(nc.vector.tensor_copy, q_raw[:], "q"), "q")
+
+        neg_top = sb.tile([P, 1], F32, name="neg_top")
+        nc.vector.tensor_scalar(neg_top[:], l1_col[:], l2_col[:], -1.0, ALU.max, ALU.mult)
+        e12 = sb.tile([P, 2], F32, name="e12")
+        nc.scalar.activation(e12[:, 0:1], l1_col[:], ACT.Exp, bias=neg_top[:])
+        nc.scalar.activation(e12[:, 1:2], l2_col[:], ACT.Exp, bias=neg_top[:])
+        total = sb.tile([P, 1], F32, name="total")
+        nc.vector.tensor_tensor(total[:], e12[:, 0:1], e12[:, 1:2], ALU.add)
+        share = sb.tile([P, 1], F32, name="share")
+        nc.vector.reciprocal(share[:], total[:])
+
+        def weights(keys_mx, factor_col, name):
+            score = ps.tile([P, 512], F32, name=name + "_score", tag="score", bufs=2)
+            multiply(score[:], q_mx, keys_mx, True, True)
+            ex = sb.tile([P, PACK, P], F32, name=name + "_exp")
+            nc.scalar.activation(ex[:], score[:].rearrange("q (p t) -> q t p", t=PACK), ACT.Exp, bias=neg_top[:])
+            scaled = sb.tile([P, PACK, P], F32, name=name + "_scaled")
+            nc.scalar.activation(scaled[:], ex[:], ACT.Copy, scale=share[:])
+            turned = ps.tile([P, PACK, P], F32, name=name + "_turned", tag="turn", bufs=2)
+            for t in range(PACK):
+                nc.tensor.transpose(turned[:, t, :], scaled[:, t, :], ident[:])
+            woven = sb.tile([P, Q * PACK], BF16, name=name + "_woven", align_bytes=64)
+            nc.vector.tensor_tensor(
+                woven[:].rearrange("p (q t) -> p q t", t=PACK),
+                turned[:].rearrange("p t q -> p q t"),
+                factor_col[:].unsqueeze(1).to_broadcast([P, Q, PACK]),
+                ALU.mult,
+            )
+            return quantize(woven, name)
+
+        key_codes = sb.tile([P, I], U32, name="key_codes", align_bytes=64)
+        nc.vector.tensor_copy(key_codes[:], key_pool[:].bitcast(U32).indirect(offsets[:]))
+        key_scales = sb.tile([P, I], U8, name="key_scales", align_bytes=64)
+        nc.vector.tensor_copy(key_scales[:], scale_pool[:].indirect(offsets[:]))
+        x_mx = weights((key_codes, key_scales), size_col, "x")
+
+        pkey_mx = quantize(weave(nc.scalar.copy, pkey_raw[:], "pkey"), "pkey")
+        w_mx = weights(pkey_mx, psz_col, "w")
+
+        acc = []
+        for b in range(BLOCKS):
+            picked = sb.tile([P, I], BF16, name="picked%d" % b)
+            nc.vector.tensor_copy(picked[:], val_pool[b][:].indirect(offsets[:]))
+            pairs = picked[:].bitcast(F32)
+            turned = ps.tile([P, 2, P], F32, name="v_turned%d" % b, tag="turn", bufs=2)
+            for u in range(2):
+                nc.tensor.transpose(turned[:, u, :], pairs[:, u : I // 2 : 2], ident[:])
+            woven = sb.tile([P, P * PACK], BF16, name="v_woven%d" % b, align_bytes=64)
+            nc.scalar.copy(
+                woven[:].bitcast(F32).rearrange("p (e u) -> p e u", u=2),
+                turned[:].rearrange("p u e -> p e u"),
+            )
+            v_mx = quantize(woven, "v%d" % b)
+            acc_b = ps.tile([P, P], F32, name="acc%d" % b)
+            multiply(acc_b[:], x_mx, v_mx, True, False)
+            acc.append(acc_b)
+
+        for h in range(2):
+            result = sb.tile([P, HALF], F32, name="result%d" % h)
+            woven = []
+            for k in range(2):
+                copy = nc.vector.tensor_copy if k == 0 else nc.scalar.copy
+                woven.append(weave(copy, pval_raw[h][:, :, k * P : (k + 1) * P], "pval%d" % (2 * h + k)))
+            for k in range(2):
+                b = 2 * h + k
+                multiply(acc[b][:], w_mx, quantize(woven[k], "pval%d" % b), False, True)
+            for k in range(2):
+                copy = nc.scalar.copy if k == 0 else nc.vector.tensor_copy
+                copy(result[:, k * P : (k + 1) * P], acc[2 * h + k][:])
+            nc.sync.dma_start(out[:, h * HALF : (h + 1) * HALF], result[:])

@@ -28,139 +28,173 @@ def tile_attend_cascade_kernel(tc, query, pkey, pval, keys_words, keys_scales, v
         sb = ctx.enter_context(tc.tile_pool(name="sb", bufs=1))
         ps = ctx.enter_context(tc.psum_pool(name="ps", bufs=1))
 
-        def weave(copy, raw, name):
-            width = raw.shape[2]
-            woven = sb.tile([P, width * PACK], BF16, name=name + "_woven", align_bytes=64)
+        def staged(shape, dtype, name, tag):
+            return sb.tile(shape, dtype, name=name, tag=tag, align_bytes=64)
+
+        def woven_tile(width, name, tag=None):
+            return staged([P, width * PACK], BF16, name + "_woven", tag or name + "_woven")[:]
+
+        def block(woven, k):
+            return woven[:, k * P * PACK : (k + 1) * P * PACK]
+
+        def weave(copy, woven, raw):
             copy(
-                woven[:].rearrange("p (c i t) -> p c t i", i=4, t=PACK),
+                woven.rearrange("p (c i t) -> p c t i", i=4, t=PACK),
                 raw.rearrange("p t (c i) -> p c t i", i=4),
             )
             return woven
 
-        def quantize(woven, name):
-            width = woven.shape[1] // PACK
-            codes = sb.tile([P, width], U32, name=name + "_codes", align_bytes=64)
+        def operand(width, name, tag=None):
+            codes = staged([P, width], U32, name + "_codes", tag or name + "_codes")
             scales = sb.tile([P, width], U8, name=name + "_scales", align_bytes=64)
-            nc.vector.quantize_mx(out=codes[:].bitcast(FP8X4), scales=scales[:], in_=woven[:])
-            return codes, scales
+            return codes[:], scales[:]
+
+        def columns(mx, lo, hi):
+            return mx[0][:, lo:hi], mx[1][:, lo:hi]
+
+        def quantize(mx, woven):
+            nc.vector.quantize_mx(out=mx[0].bitcast(FP8X4), scales=mx[1], in_=woven)
+            return mx
 
         def multiply(acc, lhs, rhs, start, stop):
             nc.tensor.matmul_mx(
                 out=acc,
-                lhsT=lhs[0][:].bitcast(FP8X4),
-                lhsT_scale=lhs[1][:],
-                rhs=rhs[0][:].bitcast(FP8X4),
-                rhs_scale=rhs[1][:],
+                lhsT=lhs[0].bitcast(FP8X4),
+                lhsT_scale=lhs[1],
+                rhs=rhs[0].bitcast(FP8X4),
+                rhs_scale=rhs[1],
                 start=start,
                 stop=stop,
             )
 
         offsets = sb.tile([P, I // 16], U16, name="offsets")
         nc.sync.dma_start(offsets[:], offs)
+        l1_col = sb.tile([P, 1], F32, name="l1_col")
+        nc.sync.dma_start(l1_col[:], l1)
+        l2_col = sb.tile([P, 1], F32, name="l2_col")
+        nc.sync.dma_start(l2_col[:], l2)
         q_raw = sb.tile([P, PACK, Q], F32, name="q_raw")
         nc.sync.dma_start(q_raw[:], query.rearrange("(p t) q -> p t q", t=PACK))
         key_pool = sb.tile([P, T], I32, name="key_pool")
         nc.sync.dma_start(key_pool[:], keys_words[0].rearrange("p n t -> p (n t)").bitcast(I32))
-        pkey_raw = sb.tile([P, PACK, M], F32, name="pkey_raw")
-        nc.sync.dma_start(pkey_raw[:], pkey.rearrange("(p t) m -> p t m", t=PACK))
-
         scale_pool = sb.tile([P, T], U8, name="scale_pool")
         nc.vector.memset(scale_pool[:].bitcast(I32), 0)
         for r in range(4):
-            nc.gpsimd.dma_start(scale_pool[r:P:32, :].bitcast(I32), keys_scales[0, r:16:4, :].bitcast(I32))
+            nc.sync.dma_start(scale_pool[r:P:32, :].bitcast(I32), keys_scales[0, r:16:4, :].bitcast(I32))
+        pkey_raw = staged([P, PACK, M], F32, "pkey_raw", "chain_pkey")
+        nc.sync.dma_start(pkey_raw[:], pkey.rearrange("(p t) m -> p t m", t=PACK))
 
-        l1_col = sb.tile([P, 1], F32, name="l1_col")
-        nc.scalar.dma_start(l1_col[:], l1)
-        l2_col = sb.tile([P, 1], F32, name="l2_col")
-        nc.scalar.dma_start(l2_col[:], l2)
-        size_col = sb.tile([P, PACK], F32, name="size_col")
-        nc.scalar.dma_start(size_col[:], size.rearrange("o (p t) -> p (o t)", t=PACK))
-        psz_col = sb.tile([P, PACK], F32, name="psz_col")
-        nc.scalar.dma_start(psz_col[:], psz.rearrange("o (p t) -> p (o t)", t=PACK))
-
-        val_pool = []
-        for b in range(BLOCKS):
-            pool_b = sb.tile([P, T], F32, name="val_pool%d" % b)
+        def load_values(b):
+            pool_b = staged([P, T], F32, "val_pool%d" % b, "chain%d" % b)
             nc.sync.dma_start(pool_b[:], vals[b * P : (b + 1) * P, :])
-            val_pool.append(pool_b)
+            return pool_b
+
+        def load_factor(row, name):
+            col = staged([P, PACK], F32, name, "chain_" + name)
+            nc.sync.dma_start(col[:], row.rearrange("o (p t) -> p (o t)", t=PACK))
+            return col
+
+        val_pool = [load_values(0)]
+        size_col = load_factor(size, "size")
+        psz_col = load_factor(psz, "psz")
+        val_pool.append(load_values(1))
+        val_pool.append(load_values(2))
+        val_pool.append(load_values(3))
         pval_rows = pval.rearrange("(p t) e -> p t e", t=PACK)
         pval_raw = []
         for h in range(2):
-            raw_h = sb.tile([P, PACK, HALF], F32, name="pval_raw%d" % h)
+            raw_h = staged([P, PACK, HALF], F32, "pval_raw%d" % h, "pval_raw%d" % h)
             nc.sync.dma_start(raw_h[:], pval_rows[:, :, h * HALF : (h + 1) * HALF])
             pval_raw.append(raw_h)
 
         ident = sb.tile([P, P], F32, name="ident")
         make_identity(nc, ident[:])
 
-        q_mx = quantize(weave(nc.vector.tensor_copy, q_raw[:], "q"), "q")
+        q_mx = quantize(operand(Q, "q"), weave(nc.vector.tensor_copy, woven_tile(Q, "q"), q_raw[:]))
 
         neg_top = sb.tile([P, 1], F32, name="neg_top")
         nc.vector.tensor_scalar(neg_top[:], l1_col[:], l2_col[:], -1.0, ALU.max, ALU.mult)
-        e12 = sb.tile([P, 2], F32, name="e12")
-        nc.scalar.activation(e12[:, 0:1], l1_col[:], ACT.Exp, bias=neg_top[:])
-        nc.scalar.activation(e12[:, 1:2], l2_col[:], ACT.Exp, bias=neg_top[:])
-        total = sb.tile([P, 1], F32, name="total")
-        nc.vector.tensor_tensor(total[:], e12[:, 0:1], e12[:, 1:2], ALU.add)
-        share = sb.tile([P, 1], F32, name="share")
-        nc.vector.reciprocal(share[:], total[:])
+        low = sb.tile([P, 1], F32, name="low")
+        nc.vector.tensor_tensor(low[:], l1_col[:], l2_col[:], ALU.min)
+        ratio = sb.tile([P, 1], F32, name="ratio")
+        nc.scalar.activation(ratio[:], low[:], ACT.Exp, bias=neg_top[:])
+        excess = sb.tile([P, 1], F32, name="excess")
+        nc.scalar.activation(excess[:], ratio[:], ACT.Ln, bias=1.0)
+        neg_lse = sb.tile([P, 1], F32, name="neg_lse")
+        nc.scalar.activation(neg_lse[:], excess[:], ACT.Identity, bias=neg_top[:], scale=-1.0)
+        warm = sb.tile([P, 1], F32, name="warm")
+        nc.scalar.activation(warm[:], excess[:], ACT.Exp)
 
-        def weights(keys_mx, factor_col, name):
-            score = ps.tile([P, 512], F32, name=name + "_score", tag="score", bufs=2)
+        def turned_weights(keys_mx, name):
+            score = ps.tile([P, 512], F32, name=name + "_score", tag=name)
             multiply(score[:], q_mx, keys_mx, True, True)
             ex = sb.tile([P, PACK, P], F32, name=name + "_exp")
-            nc.scalar.activation(ex[:], score[:].rearrange("q (p t) -> q t p", t=PACK), ACT.Exp, bias=neg_top[:])
-            scaled = sb.tile([P, PACK, P], F32, name=name + "_scaled")
-            nc.scalar.activation(scaled[:], ex[:], ACT.Copy, scale=share[:])
-            turned = ps.tile([P, PACK, P], F32, name=name + "_turned", tag="turn", bufs=2)
+            nc.scalar.activation(ex[:], score[:].rearrange("q (p t) -> q t p", t=PACK), ACT.Exp, bias=neg_lse[:])
+            turned = ps.tile([P, PACK, P], F32, name=name + "_turned", tag=name)
             for t in range(PACK):
-                nc.tensor.transpose(turned[:, t, :], scaled[:, t, :], ident[:])
-            woven = sb.tile([P, Q * PACK], BF16, name=name + "_woven", align_bytes=64)
+                nc.tensor.transpose(turned[:, t, :], ex[:, t, :], ident[:])
+            return turned
+
+        def weights(turned, factor_col, woven):
             nc.vector.tensor_tensor(
-                woven[:].rearrange("p (q t) -> p q t", t=PACK),
+                woven.rearrange("p (q t) -> p q t", t=PACK),
                 turned[:].rearrange("p t q -> p q t"),
                 factor_col[:].unsqueeze(1).to_broadcast([P, Q, PACK]),
                 ALU.mult,
             )
-            return quantize(woven, name)
+
+        def listed_values(b, tag):
+            picked = staged([P, I], BF16, "picked%d" % b, tag)
+            nc.vector.tensor_copy(picked[:], val_pool[b][:].indirect(offsets[:]))
+            return picked
+
+        def turn_values(picked, b, bank, woven):
+            pairs = picked[:].bitcast(F32)
+            turned = ps.tile([P, 2, P], F32, name="v_turned%d" % b, tag=bank)
+            for u in range(2):
+                nc.tensor.transpose(turned[:, u, :], pairs[:, u : I // 2 : 2], ident[:])
+            nc.scalar.copy(
+                woven.bitcast(F32).rearrange("p (e u) -> p e u", u=2),
+                turned[:].rearrange("p u e -> p e u"),
+            )
 
         key_codes = sb.tile([P, I], U32, name="key_codes", align_bytes=64)
         nc.vector.tensor_copy(key_codes[:], key_pool[:].bitcast(U32).indirect(offsets[:]))
         key_scales = sb.tile([P, I], U8, name="key_scales", align_bytes=64)
         nc.vector.tensor_copy(key_scales[:], scale_pool[:].indirect(offsets[:]))
-        x_mx = weights((key_codes, key_scales), size_col, "x")
+        x_turned = turned_weights((key_codes[:], key_scales[:]), "x")
+        pkey_woven = weave(nc.vector.tensor_copy, woven_tile(M, "pkey"), pkey_raw[:])
+        w_turned = turned_weights(quantize(operand(M, "pkey"), pkey_woven), "w")
 
-        pkey_mx = quantize(weave(nc.scalar.copy, pkey_raw[:], "pkey"), "pkey")
-        w_mx = weights(pkey_mx, psz_col, "w")
+        picked0 = listed_values(0, "chain_pkey")
+        early_woven = woven_tile(4 * P, "early", "chain0")
+        weights(x_turned, size_col, block(early_woven, 0))
+        turn_values(picked0, 0, "x", block(early_woven, 2))
+        picked1 = listed_values(1, "chain_size")
+        weights(w_turned, psz_col, block(early_woven, 1))
+        turn_values(picked1, 1, "w", block(early_woven, 3))
+        v23_woven = woven_tile(HALF, "v23")
+        turn_values(listed_values(2, "chain_psz"), 2, "v2", block(v23_woven, 0))
+        early_mx = quantize(operand(4 * P, "early", "chain2"), early_woven)
+        x_mx, w_mx = columns(early_mx, 0, Q), columns(early_mx, Q, 2 * Q)
+        acc_a = ps.tile([P, HALF], F32, name="acc_a")
+        multiply(acc_a[:], x_mx, columns(early_mx, 2 * P, 4 * P), True, False)
+        turn_values(listed_values(3, "chain0"), 3, "v3", block(v23_woven, 1))
 
-        acc = []
-        for b in range(BLOCKS):
-            picked = sb.tile([P, I], BF16, name="picked%d" % b)
-            nc.vector.tensor_copy(picked[:], val_pool[b][:].indirect(offsets[:]))
-            pairs = picked[:].bitcast(F32)
-            turned = ps.tile([P, 2, P], F32, name="v_turned%d" % b, tag="turn", bufs=2)
-            for u in range(2):
-                nc.tensor.transpose(turned[:, u, :], pairs[:, u : I // 2 : 2], ident[:])
-            woven = sb.tile([P, P * PACK], BF16, name="v_woven%d" % b, align_bytes=64)
-            nc.scalar.copy(
-                woven[:].bitcast(F32).rearrange("p (e u) -> p e u", u=2),
-                turned[:].rearrange("p u e -> p e u"),
-            )
-            v_mx = quantize(woven, "v%d" % b)
-            acc_b = ps.tile([P, P], F32, name="acc%d" % b)
-            multiply(acc_b[:], x_mx, v_mx, True, False)
-            acc.append(acc_b)
-
-        for h in range(2):
-            result = sb.tile([P, HALF], F32, name="result%d" % h)
-            woven = []
-            for k in range(2):
-                copy = nc.vector.tensor_copy if k == 0 else nc.scalar.copy
-                woven.append(weave(copy, pval_raw[h][:, :, k * P : (k + 1) * P], "pval%d" % (2 * h + k)))
-            for k in range(2):
-                b = 2 * h + k
-                multiply(acc[b][:], w_mx, quantize(woven[k], "pval%d" % b), False, True)
-            for k in range(2):
-                copy = nc.scalar.copy if k == 0 else nc.vector.tensor_copy
-                copy(result[:, k * P : (k + 1) * P], acc[2 * h + k][:])
-            nc.sync.dma_start(out[:, h * HALF : (h + 1) * HALF], result[:])
+        a_woven = weave(nc.vector.tensor_copy, woven_tile(HALF, "pval_a", "chain3"), pval_raw[0][:])
+        multiply(acc_a[:], w_mx, quantize(operand(HALF, "pval_a"), a_woven), False, True)
+        b_woven = woven_tile(HALF, "pval_b", "pval_raw0")
+        weave(nc.vector.tensor_copy, block(b_woven, 0), pval_raw[1][:, :, 0:P])
+        weave(nc.scalar.copy, block(b_woven, 1), pval_raw[1][:, :, P:HALF])
+        result_a = staged([P, HALF], F32, "result_a", "pval_raw1")
+        nc.scalar.copy(result_a[:], acc_a[:])
+        nc.sync.dma_start(out[:, 0:HALF], result_a[:])
+        v23_mx = quantize(operand(HALF, "v23", "chain3"), v23_woven)
+        b_mx = quantize(operand(HALF, "pval_b"), b_woven)
+        result_b = sb.tile([P, HALF], F32, name="result_b")
+        for k, (bank, copy) in enumerate((("acc0", nc.scalar.copy), ("acc1", nc.vector.tensor_copy))):
+            acc = ps.tile([P, P], F32, name="acc%d" % k, tag=bank)
+            multiply(acc[:], x_mx, columns(v23_mx, k * P, (k + 1) * P), True, False)
+            multiply(acc[:], w_mx, columns(b_mx, k * P, (k + 1) * P), False, True)
+            copy(result_b[:, k * P : (k + 1) * P], acc[:])
+        nc.sync.dma_start(out[:, HALF:E], result_b[:])

@@ -20,6 +20,7 @@ P = 128
 PACK = 4
 BLOCKS = E // P
 HALF = E // 2
+SPLIT = 192
 
 
 def tile_attend_cascade_kernel(tc, query, pkey, pval, keys_words, keys_scales, vals, l1, l2, psz, size, offs, out):
@@ -96,8 +97,8 @@ def tile_attend_cascade_kernel(tc, query, pkey, pval, keys_words, keys_scales, v
 
         val_pool = [load_values(0)]
         size_col = load_factor(size, "size")
-        psz_col = load_factor(psz, "psz")
         val_pool.append(load_values(1))
+        psz_col = load_factor(psz, "psz")
         val_pool.append(load_values(2))
         val_pool.append(load_values(3))
         pval_rows = pval.rearrange("(p t) e -> p t e", t=PACK)
@@ -143,14 +144,11 @@ def tile_attend_cascade_kernel(tc, query, pkey, pval, keys_words, keys_scales, v
                 ALU.mult,
             )
 
-        def listed_values(b, tag):
-            picked = staged([P, I], BF16, "picked%d" % b, tag)
+        def listed_values(b, woven):
+            picked = sb.tile([P, I], BF16, name="picked%d" % b)
             nc.vector.tensor_copy(picked[:], val_pool[b][:].indirect(offsets[:]))
-            return picked
-
-        def turn_values(picked, b, bank, woven):
             pairs = picked[:].bitcast(F32)
-            turned = ps.tile([P, 2, P], F32, name="v_turned%d" % b, tag=bank)
+            turned = ps.tile([P, 2, P], F32, name="v_turned%d" % b, tag="v_turned", bufs=3)
             for u in range(2):
                 nc.tensor.transpose(turned[:, u, :], pairs[:, u : I // 2 : 2], ident[:])
             nc.scalar.copy(
@@ -163,33 +161,31 @@ def tile_attend_cascade_kernel(tc, query, pkey, pval, keys_words, keys_scales, v
         key_scales = sb.tile([P, I], U8, name="key_scales", align_bytes=64)
         nc.vector.tensor_copy(key_scales[:], scale_pool[:].indirect(offsets[:]))
         x_turned = turned_weights((key_codes[:], key_scales[:]), "x")
-        pkey_woven = weave(nc.vector.tensor_copy, woven_tile(M, "pkey"), pkey_raw[:])
+        pkey_woven = weave(nc.vector.tensor_copy, woven_tile(M, "pkey", "chain_early"), pkey_raw[:])
         w_turned = turned_weights(quantize(operand(M, "pkey"), pkey_woven), "w")
 
-        picked0 = listed_values(0, "chain_pkey")
-        early_woven = woven_tile(4 * P, "early", "chain0")
+        early_woven = woven_tile(4 * P, "early")
+        listed_values(0, block(early_woven, 2))
         weights(x_turned, size_col, block(early_woven, 0))
-        turn_values(picked0, 0, "x", block(early_woven, 2))
-        picked1 = listed_values(1, "chain_size")
+        listed_values(1, block(early_woven, 3))
         weights(w_turned, psz_col, block(early_woven, 1))
-        turn_values(picked1, 1, "w", block(early_woven, 3))
         v23_woven = woven_tile(HALF, "v23")
-        turn_values(listed_values(2, "chain_psz"), 2, "v2", block(v23_woven, 0))
+        listed_values(2, block(v23_woven, 0))
         early_mx = quantize(operand(4 * P, "early", "chain2"), early_woven)
         x_mx, w_mx = columns(early_mx, 0, Q), columns(early_mx, Q, 2 * Q)
         acc_a = ps.tile([P, HALF], F32, name="acc_a")
         multiply(acc_a[:], x_mx, columns(early_mx, 2 * P, 4 * P), True, False)
-        turn_values(listed_values(3, "chain0"), 3, "v3", block(v23_woven, 1))
+        listed_values(3, block(v23_woven, 1))
 
-        a_woven = weave(nc.vector.tensor_copy, woven_tile(HALF, "pval_a", "chain3"), pval_raw[0][:])
+        a_woven = weave(nc.vector.tensor_copy, woven_tile(HALF, "pval_a", "chain_a"), pval_raw[0][:])
         multiply(acc_a[:], w_mx, quantize(operand(HALF, "pval_a"), a_woven), False, True)
-        b_woven = woven_tile(HALF, "pval_b", "pval_raw0")
-        weave(nc.vector.tensor_copy, block(b_woven, 0), pval_raw[1][:, :, 0:P])
-        weave(nc.scalar.copy, block(b_woven, 1), pval_raw[1][:, :, P:HALF])
+        b_woven = woven_tile(HALF, "pval_b")
+        weave(nc.vector.tensor_copy, b_woven[:, 0 : SPLIT * PACK], pval_raw[1][:, :, 0:SPLIT])
+        weave(nc.scalar.copy, b_woven[:, SPLIT * PACK :], pval_raw[1][:, :, SPLIT:HALF])
         result_a = staged([P, HALF], F32, "result_a", "pval_raw1")
         nc.scalar.copy(result_a[:], acc_a[:])
         nc.sync.dma_start(out[:, 0:HALF], result_a[:])
-        v23_mx = quantize(operand(HALF, "v23", "chain3"), v23_woven)
+        v23_mx = quantize(operand(HALF, "v23", "chain_a"), v23_woven)
         b_mx = quantize(operand(HALF, "pval_b"), b_woven)
         result_b = sb.tile([P, HALF], F32, name="result_b")
         for k, (bank, copy) in enumerate((("acc0", nc.scalar.copy), ("acc1", nc.vector.tensor_copy))):

from contextlib import ExitStack

import concourse.mybir as mybir
from concourse.masks import make_identity

D, T, I, Q, E, M = 512, 2048, 512, 128, 512, 512
FLOPS = 2 * Q * (D * M + D * I + M * E + I * E)

F32 = mybir.dt.float32
BF16 = mybir.dt.bfloat16
I32 = mybir.dt.int32
U32 = mybir.dt.uint32
U16 = mybir.dt.uint16
U8 = mybir.dt.uint8
FP8X4 = mybir.dt.float8_e4m3fn_x4
ALU = mybir.AluOpType
ACT = mybir.ActivationFunctionType

P = 128
PACK = 4
BLOCKS = E // P
HALF = E // 2
SPLIT = 192


def tile_attend_cascade_kernel(tc, query, pkey, pval, keys_words, keys_scales, vals, l1, l2, psz, size, offs, out):
    nc = tc.nc
    with ExitStack() as ctx:
        sb = ctx.enter_context(tc.tile_pool(name="sb", bufs=1))
        ps = ctx.enter_context(tc.psum_pool(name="ps", bufs=1))

        def staged(shape, dtype, name, tag):
            return sb.tile(shape, dtype, name=name, tag=tag, align_bytes=64)

        def woven_tile(width, name, tag=None):
            return staged([P, width * PACK], BF16, name + "_woven", tag or name + "_woven")[:]

        def block(woven, k):
            return woven[:, k * P * PACK : (k + 1) * P * PACK]

        def weave(copy, woven, raw):
            copy(
                woven.rearrange("p (c i t) -> p c t i", i=4, t=PACK),
                raw.rearrange("p t (c i) -> p c t i", i=4),
            )
            return woven

        def operand(width, name, tag=None):
            codes = staged([P, width], U32, name + "_codes", tag or name + "_codes")
            scales = sb.tile([P, width], U8, name=name + "_scales", align_bytes=64)
            return codes[:], scales[:]

        def columns(mx, lo, hi):
            return mx[0][:, lo:hi], mx[1][:, lo:hi]

        def quantize(mx, woven):
            nc.vector.quantize_mx(out=mx[0].bitcast(FP8X4), scales=mx[1], in_=woven)
            return mx

        def multiply(acc, lhs, rhs, start, stop):
            nc.tensor.matmul_mx(
                out=acc,
                lhsT=lhs[0].bitcast(FP8X4),
                lhsT_scale=lhs[1],
                rhs=rhs[0].bitcast(FP8X4),
                rhs_scale=rhs[1],
                start=start,
                stop=stop,
            )

        offsets = sb.tile([P, I // 16], U16, name="offsets")
        nc.sync.dma_start(offsets[:], offs)
        l1_col = sb.tile([P, 1], F32, name="l1_col")
        nc.sync.dma_start(l1_col[:], l1)
        l2_col = sb.tile([P, 1], F32, name="l2_col")
        nc.sync.dma_start(l2_col[:], l2)
        q_raw = sb.tile([P, PACK, Q], F32, name="q_raw")
        nc.sync.dma_start(q_raw[:], query.rearrange("(p t) q -> p t q", t=PACK))
        key_pool = sb.tile([P, T], I32, name="key_pool")
        nc.sync.dma_start(key_pool[:], keys_words[0].rearrange("p n t -> p (n t)").bitcast(I32))
        scale_pool = sb.tile([P, T], U8, name="scale_pool")
        nc.vector.memset(scale_pool[:].bitcast(I32), 0)
        for r in range(4):
            nc.sync.dma_start(scale_pool[r:P:32, :].bitcast(I32), keys_scales[0, r:16:4, :].bitcast(I32))
        pkey_raw = staged([P, PACK, M], F32, "pkey_raw", "chain_pkey")
        nc.sync.dma_start(pkey_raw[:], pkey.rearrange("(p t) m -> p t m", t=PACK))

        def load_values(b):
            pool_b = staged([P, T], F32, "val_pool%d" % b, "chain%d" % b)
            nc.sync.dma_start(pool_b[:], vals[b * P : (b + 1) * P, :])
            return pool_b

        def load_factor(row, name):
            col = staged([P, PACK], F32, name, "chain_" + name)
            nc.sync.dma_start(col[:], row.rearrange("o (p t) -> p (o t)", t=PACK))
            return col

        val_pool = [load_values(0)]
        size_col = load_factor(size, "size")
        val_pool.append(load_values(1))
        psz_col = load_factor(psz, "psz")
        val_pool.append(load_values(2))
        val_pool.append(load_values(3))
        pval_rows = pval.rearrange("(p t) e -> p t e", t=PACK)
        pval_raw = []
        for h in range(2):
            raw_h = staged([P, PACK, HALF], F32, "pval_raw%d" % h, "pval_raw%d" % h)
            nc.sync.dma_start(raw_h[:], pval_rows[:, :, h * HALF : (h + 1) * HALF])
            pval_raw.append(raw_h)

        ident = sb.tile([P, P], F32, name="ident")
        make_identity(nc, ident[:])

        q_mx = quantize(operand(Q, "q"), weave(nc.vector.tensor_copy, woven_tile(Q, "q"), q_raw[:]))

        neg_top = sb.tile([P, 1], F32, name="neg_top")
        nc.vector.tensor_scalar(neg_top[:], l1_col[:], l2_col[:], -1.0, ALU.max, ALU.mult)
        low = sb.tile([P, 1], F32, name="low")
        nc.vector.tensor_tensor(low[:], l1_col[:], l2_col[:], ALU.min)
        ratio = sb.tile([P, 1], F32, name="ratio")
        nc.scalar.activation(ratio[:], low[:], ACT.Exp, bias=neg_top[:])
        excess = sb.tile([P, 1], F32, name="excess")
        nc.scalar.activation(excess[:], ratio[:], ACT.Ln, bias=1.0)
        neg_lse = sb.tile([P, 1], F32, name="neg_lse")
        nc.scalar.activation(neg_lse[:], excess[:], ACT.Identity, bias=neg_top[:], scale=-1.0)
        warm = sb.tile([P, 1], F32, name="warm")
        nc.scalar.activation(warm[:], excess[:], ACT.Exp)

        def turned_weights(keys_mx, name):
            score = ps.tile([P, 512], F32, name=name + "_score", tag=name)
            multiply(score[:], q_mx, keys_mx, True, True)
            ex = sb.tile([P, PACK, P], F32, name=name + "_exp")
            nc.scalar.activation(ex[:], score[:].rearrange("q (p t) -> q t p", t=PACK), ACT.Exp, bias=neg_lse[:])
            turned = ps.tile([P, PACK, P], F32, name=name + "_turned", tag=name)
            for t in range(PACK):
                nc.tensor.transpose(turned[:, t, :], ex[:, t, :], ident[:])
            return turned

        def weights(turned, factor_col, woven):
            nc.vector.tensor_tensor(
                woven.rearrange("p (q t) -> p q t", t=PACK),
                turned[:].rearrange("p t q -> p q t"),
                factor_col[:].unsqueeze(1).to_broadcast([P, Q, PACK]),
                ALU.mult,
            )

        def listed_values(b, woven):
            picked = sb.tile([P, I], BF16, name="picked%d" % b)
            nc.vector.tensor_copy(picked[:], val_pool[b][:].indirect(offsets[:]))
            pairs = picked[:].bitcast(F32)
            turned = ps.tile([P, 2, P], F32, name="v_turned%d" % b, tag="v_turned", bufs=3)
            for u in range(2):
                nc.tensor.transpose(turned[:, u, :], pairs[:, u : I // 2 : 2], ident[:])
            nc.scalar.copy(
                woven.bitcast(F32).rearrange("p (e u) -> p e u", u=2),
                turned[:].rearrange("p u e -> p e u"),
            )

        key_codes = sb.tile([P, I], U32, name="key_codes", align_bytes=64)
        nc.vector.tensor_copy(key_codes[:], key_pool[:].bitcast(U32).indirect(offsets[:]))
        key_scales = sb.tile([P, I], U8, name="key_scales", align_bytes=64)
        nc.vector.tensor_copy(key_scales[:], scale_pool[:].indirect(offsets[:]))
        x_turned = turned_weights((key_codes[:], key_scales[:]), "x")
        pkey_woven = weave(nc.vector.tensor_copy, woven_tile(M, "pkey", "chain_early"), pkey_raw[:])
        w_turned = turned_weights(quantize(operand(M, "pkey"), pkey_woven), "w")

        early_woven = woven_tile(4 * P, "early")
        listed_values(0, block(early_woven, 2))
        weights(x_turned, size_col, block(early_woven, 0))
        listed_values(1, block(early_woven, 3))
        weights(w_turned, psz_col, block(early_woven, 1))
        v23_woven = woven_tile(HALF, "v23")
        listed_values(2, block(v23_woven, 0))
        early_mx = quantize(operand(4 * P, "early", "chain2"), early_woven)
        x_mx, w_mx = columns(early_mx, 0, Q), columns(early_mx, Q, 2 * Q)
        acc_a = ps.tile([P, HALF], F32, name="acc_a")
        multiply(acc_a[:], x_mx, columns(early_mx, 2 * P, 4 * P), True, False)
        listed_values(3, block(v23_woven, 1))

        a_woven = weave(nc.vector.tensor_copy, woven_tile(HALF, "pval_a", "chain_a"), pval_raw[0][:])
        multiply(acc_a[:], w_mx, quantize(operand(HALF, "pval_a"), a_woven), False, True)
        b_woven = woven_tile(HALF, "pval_b")
        weave(nc.vector.tensor_copy, b_woven[:, 0 : SPLIT * PACK], pval_raw[1][:, :, 0:SPLIT])
        weave(nc.scalar.copy, b_woven[:, SPLIT * PACK :], pval_raw[1][:, :, SPLIT:HALF])
        result_a = staged([P, HALF], F32, "result_a", "pval_raw1")
        nc.scalar.copy(result_a[:], acc_a[:])
        nc.sync.dma_start(out[:, 0:HALF], result_a[:])
        v23_mx = quantize(operand(HALF, "v23", "chain_a"), v23_woven)
        b_mx = quantize(operand(HALF, "pval_b"), b_woven)
        result_b = sb.tile([P, HALF], F32, name="result_b")
        for k, (bank, copy) in enumerate((("acc0", nc.scalar.copy), ("acc1", nc.vector.tensor_copy))):
            acc = ps.tile([P, P], F32, name="acc%d" % k, tag=bank)
            multiply(acc[:], x_mx, columns(v23_mx, k * P, (k + 1) * P), True, False)
            multiply(acc[:], w_mx, columns(b_mx, k * P, (k + 1) * P), False, True)
            copy(result_b[:, k * P : (k + 1) * P], acc[:])
        nc.sync.dma_start(out[:, HALF:E], result_b[:])
